import numpy as np
import ml_dtypes


def mxq(x, axis, fmt="e4m3"):
    dtype, down = {"e4m3": (ml_dtypes.float8_e4m3fn, 7), "e5m2": (ml_dtypes.float8_e5m2, 14)}[fmt]
    v = np.moveaxis(np.asarray(x, np.float32).astype(ml_dtypes.bfloat16).astype(np.float64), axis, -1)
    blocks = v.reshape(v.shape[:-1] + (-1, 32))
    amax = np.abs(blocks).max(-1, keepdims=True)
    byte = np.maximum(np.where(amax > 0, np.frexp(amax)[1] - 1 + 127, 0) - down, 1)
    scale = np.exp2(byte - 127.0)
    codes = (blocks / scale).astype(np.float32).astype(dtype).astype(np.float64)
    return np.moveaxis((codes * scale).reshape(v.shape), -1, axis)


WIDE = False


def mx_kscale(k):
    if not WIDE:
        return np.ones(k)
    levels = np.array([10, -10, 5, -5, 0])
    if k % 512:
        return np.exp2(np.random.permutation(np.resize(levels, k // 32))).repeat(32)
    a = np.empty((k // 512, 16))
    for p in range(k // 512):
        a[p, :8] = np.random.permutation(np.resize(levels, 8))
        for g in range(8):
            far = levels[np.abs(levels - a[p, g]) >= 10]
            a[p, g + 8] = far[np.random.randint(len(far))]
    return np.exp2(a.ravel()).repeat(32)


def f64(x):
    return np.asarray(x).astype(np.float64)


def striped(idx):
    return np.tile(idx.reshape(-1, 16).T, (8, 1)).astype(np.uint16)


def unstriped(offs):
    return offs[:16].T.reshape(-1).astype(np.int64)


E2M1 = np.array([0.0, 0.5, 1.0, 1.5, 2.0, 3.0, 4.0, 6.0, -0.0, -0.5, -1.0, -1.5, -2.0, -3.0, -4.0, -6.0])


def pack_weight(w, fmt):
    k, n = w.shape
    w = f64(np.asarray(w, np.float32).astype(ml_dtypes.bfloat16)).reshape(k // 32, 32, n)
    amax = np.abs(w).max(1)
    if fmt == "e4m3":
        byte = np.frexp(amax)[1] - 1 + 127 - 7
    else:
        mant, ex = np.frexp(amax / 6.0)
        byte = np.where(mant > 0.5, ex, ex - 1) + 127
    byte = np.clip(np.where(amax > 0, byte, 1), 1, 254)
    scaled = (w * np.exp2(127.0 - byte)[:, None, :]).reshape(k, n).astype(np.float32)
    by_word = np.ascontiguousarray(scaled.reshape(k // 512, 128, 4, n).transpose(0, 1, 3, 2))
    if fmt == "e4m3":
        words = by_word.astype(ml_dtypes.float8_e4m3fn).view(np.uint8)
    else:
        c = by_word.astype(ml_dtypes.float4_e2m1fn).view(np.uint8) & 0xF
        words = (c[..., 0::2] | (c[..., 1::2] << 4)).reshape(k // 512, 128, 2 * n)
    return np.ascontiguousarray(words), np.ascontiguousarray(byte.astype(np.uint8).reshape(k // 512, 16, n))


def unpack_weight(words, scales, fmt):
    g, _, n = scales.shape
    words = np.ascontiguousarray(words).reshape(g, 128, n, -1)
    if fmt == "e4m3":
        vals = words.view(ml_dtypes.float8_e4m3fn).astype(np.float64)
    else:
        nib = np.empty((g, 128, n, 4), np.uint8)
        nib[..., 0::2] = words & 0xF
        nib[..., 1::2] = words >> 4
        vals = E2M1[nib]
    vals = vals * np.repeat(np.exp2(scales.astype(np.float64) - 127.0), 8, axis=1)[..., None]
    return vals.transpose(0, 1, 3, 2).reshape(g * 512, n)


def gelu(v):
    return 0.5 * v * (1.0 + np.tanh(np.sqrt(2.0 / np.pi) * (v + 0.044715 * v**3)))


K, H, T, S, T2, P = 1024, 512, 4096, 1024, 2048, 1024

def setup_inputs():
    n = np.random.standard_normal
    s = mx_kscale(K)[:, None]
    u = mx_kscale(H)[:, None]
    tab_words, tab_scales = pack_weight(n((K, T)) * s, "e4m3")
    w1 = (n((K, H)) / s * u.T / np.sqrt(K)).astype(np.float32)
    w2_words, w2_scales = pack_weight(n((K, H)) / s * u.T / np.sqrt(K), "e2m1")
    w3_words, w3_scales = pack_weight(n((K, H)) / s * u.T / np.sqrt(K), "e4m3")
    w4 = (n((H, H)) / u * u.T / np.sqrt(H)).astype(np.float32)
    return {
        "tab_words": tab_words, "tab_scales": tab_scales,
        "offs": striped(np.random.permutation(T)[:S]),
        "offs2": striped(np.random.permutation(T2)[:S]),
        "offs3": striped(np.random.permutation(T2)[:P]),
        "offs4": striped(np.random.permutation(T2)[:P]),
        "w1": w1, "w2_words": w2_words, "w2_scales": w2_scales,
        "w3_words": w3_words, "w3_scales": w3_scales, "w4": w4,
        "page0": (n((H, T2)) * u).astype(np.float32),
        "slack": ((0.45 + 0.7 * n((H, P))) * u).astype(np.float32),
        "gain": np.exp(0.3 * n(H)).astype(np.float32),
        "wgs": np.exp(0.3 * n((128, S))).astype(np.float32),
        "wgo": np.exp(0.3 * n((128, P))).astype(np.float32),
    }

def reference(tab_words, tab_scales, offs, offs2, offs3, offs4, w1, w2_words, w2_scales, w3_words, w3_scales, w4, page0, slack, gain, wgs, wgo):
    v = unpack_weight(tab_words, tab_scales, "e4m3")[:, unstriped(offs)]
    h1 = mxq(f64(w1), 0, "e4m3").T @ v
    h2 = unpack_weight(w2_words, w2_scales, "e2m1").T @ v
    h3 = unpack_weight(w3_words, w3_scales, "e4m3").T @ v
    h = np.maximum(np.maximum(h1, h2), h3)
    page = f64(page0).copy()
    page[:, unstriped(offs2)] = np.tile(f64(wgs), (H // 128, 1)) * h
    x = page[:, unstriped(offs3)] - f64(slack)
    e = mxq(f64(w4), 0, "e4m3").T @ mxq(x, 0, "e4m3")
    y = np.abs(e) * f64(gain)[:, None]
    page[:, unstriped(offs4)] = np.tile(f64(wgo), (H // 128, 1)) * y
    return page

@@ -1,0 +1,345 @@
+from contextlib import ExitStack
+
+import concourse.mybir as mybir
+from concourse.masks import make_identity
+
+K, H, T, S, T2, J = 1024, 512, 4096, 1024, 2048, 1024
+FLOPS = 2 * (3 * K * H * S + H * H * J)
+
+F32 = mybir.dt.float32
+BF16 = mybir.dt.bfloat16
+I32 = mybir.dt.int32
+U32 = mybir.dt.uint32
+U16 = mybir.dt.uint16
+U8 = mybir.dt.uint8
+FP8X4 = mybir.dt.float8_e4m3fn_x4
+FP4X4 = mybir.dt.float4_e2m1fn_x4
+ALU = mybir.AluOpType
+ACT = mybir.ActivationFunctionType
+
+P = 128
+PACK = 4
+PASSES = K // (P * PACK)
+TILES = H // P
+BANK = 512
+HALVES = S // BANK
+PER_COL = 16
+FIRST = 256
+REST = J - FIRST
+
+
+def tile_list_wake_loading_page_kernel(
+    tc, tab_words, tab_scales, offs, offs2, offs3, offs4, w1, w2_words, w2_scales,
+    w3_words, w3_scales, w4, page0, slack, gain, wgs, wgo, out,
+):
+    nc = tc.nc
+    with ExitStack() as ctx:
+        lists = ctx.enter_context(tc.tile_pool(name="lists", bufs=1))
+        keep = ctx.enter_context(tc.tile_pool(name="keep", bufs=1))
+        ring = ctx.enter_context(tc.tile_pool(name="ring", bufs=2))
+        psum = ctx.enter_context(tc.psum_pool(name="psum", bufs=1))
+
+        def held(shape, dtype, name, tag=None):
+            return keep.tile(shape, dtype, name=name, tag=tag or name, align_bytes=64)
+
+        def bank(b, name):
+            return psum.tile([P, BANK], F32, name=name, tag=f"bank{b}")
+
+        def load_list(dram, name):
+            tile = lists.tile([P, dram.shape[1]], U16, name=name)
+            nc.sync.dma_start(tile[:], dram)
+            return tile
+
+        def entries(tile, first, count):
+            if count == tile.shape[1] * PER_COL:
+                return tile[:]
+            return tile[:, first // PER_COL : (first + count) // PER_COL]
+
+        def load_planes(queue, zeroing, dram, name):
+            width = dram.shape[2]
+            tile = held([P, PASSES, width], U8, name)
+            zeroing.memset(tile[:].bitcast(I32), 0)
+            for q in range(4):
+                queue.dma_start(
+                    out=tile[32 * q : 32 * q + 4].bitcast(I32),
+                    in_=dram[:, 4 * q : 4 * q + 4, :].rearrange("a r c -> r a c").bitcast(I32),
+                )
+            return tile
+
+        def load_w1(first, count):
+            raw = held([P, PASSES, PACK, count], F32, f"w1_raw{first}")
+            for a in range(PASSES):
+                rows = w1[a * P * PACK : (a + 1) * P * PACK, first : first + count]
+                nc.sync.dma_start(out=raw[:, a], in_=rows.rearrange("(p i) c -> p i c", i=PACK))
+            return raw
+
+        def load_words(dram, per_col, first, count, name):
+            tile = held([P, PASSES, count * per_col], U8, name)
+            nc.sync.dma_start(
+                out=tile[:].bitcast(I32),
+                in_=dram[:, :, first * per_col : (first + count) * per_col].rearrange("a p c -> p a c").bitcast(I32),
+            )
+            return tile
+
+        def load_rows(dram, t, name):
+            tile = held([P, dram.shape[1]], F32, name)
+            nc.sync.dma_start(out=tile[:], in_=dram[t * P : (t + 1) * P, :])
+            return tile
+
+        def interleave(dst, src):
+            nc.scalar.copy(
+                out=dst.rearrange("p (c n) i -> p c i n", n=4),
+                in_=src.rearrange("p i (c n) -> p c i n", n=4),
+            )
+
+        def quantise(grouped, width, name, tag=None):
+            codes = held([P, width], U32, name + "_codes", tag)
+            scales = held([P, width], U8, name + "_scales")
+            nc.vector.quantize_mx(out=codes[:].bitcast(FP8X4), scales=scales[:], in_=grouped)
+            return codes, scales
+
+        w3_flat = w3_words.rearrange("a p c i -> a p (c i)")
+        idx = load_list(offs, "idx")
+        w_rows = held([4, 2, PASSES, 4, H], U8, "w_rows")
+        for w, dram in enumerate((w2_scales, w3_scales)):
+            nc.sync.dma_start(
+                out=w_rows[:, w].rearrange("r a q c -> r (a q) c").bitcast(I32),
+                in_=dram.rearrange("a (q r) c -> r (a q) c", r=4).bitcast(I32),
+            )
+        idx2 = load_list(offs2, "idx2")
+        w1_raw = [load_w1(0, P)]
+        w3_first = load_words(w3_flat, 4, 0, P, "w3_first")
+        w2_first = load_words(w2_words, 2, 0, P, "w2_first")
+        tab_planes = load_planes(nc.sync, nc.vector, tab_scales, "tab_planes")
+        w_planes = held([P, 2, PASSES, H], U8, "w_planes")
+        nc.vector.memset(w_planes[:].rearrange("p w a c -> p (w a c)").bitcast(I32), 0)
+        for q in range(4):
+            nc.vector.tensor_copy(
+                out=w_planes[32 * q : 32 * q + 4].rearrange("r w a c -> r (w a) c").bitcast(I32),
+                in_=w_rows[:, :, :, q, :].rearrange("r w a c -> r (w a) c").bitcast(I32),
+            )
+        w2_planes, w3_planes = w_planes[:, 0], w_planes[:, 1]
+        ident = held([P, P], F32, "ident")
+        make_identity(nc, ident[:])
+
+        table = []
+        for a in range(PASSES):
+            words = held([P, T], U32, f"table{a}")
+            nc.sync.dma_start(
+                out=words[:].bitcast(I32), in_=tab_words[a].rearrange("p t i -> p (t i)").bitcast(I32)
+            )
+            table.append(words)
+
+        page = [None] * TILES
+        neg_slack = [None] * TILES
+        page[0] = load_rows(page0, 0, "page_0")
+        wgs_sb = held([P, S], F32, "wgs_sb", "after_first_writing")
+        nc.sync.dma_start(out=wgs_sb[:, :BANK], in_=wgs[:, :BANK])
+        w1_raw.append(load_w1(P, P))
+        w3_rest = load_words(w3_flat, 4, P, H - P, "w3_rest")
+        w2_rest = load_words(w2_words, 2, P, H - P, "w2_rest")
+        nc.sync.dma_start(out=wgs_sb[:, BANK:], in_=wgs[:, BANK:])
+        idx3 = load_list(offs3, "idx3")
+        w1_raw.append(load_w1(2 * P, 2 * P))
+        page[1] = load_rows(page0, 1, "page_1")
+        neg_slack[0] = load_rows(slack, 0, "slack_0")
+        w4_raw = held([P, PACK, H], F32, "w4_raw")
+        nc.sync.dma_start(out=w4_raw[:], in_=w4.rearrange("(p i) n -> p i n", i=PACK))
+        page[2] = load_rows(page0, 2, "page_2")
+        for t in range(1, TILES):
+            neg_slack[t] = load_rows(slack, t, f"slack_{t}")
+        wgo_sb = load_rows(wgo, 0, "wgo_sb")
+        idx4 = load_list(offs4, "idx4")
+        gain_sb = held([P, TILES], F32, "gain_sb")
+        with nc.allow_non_contiguous_dma(reason="one gain a partition and row tile"):
+            nc.sync.dma_start(out=gain_sb[:], in_=gain.rearrange("(t p) -> p t", p=P))
+        page[3] = load_rows(page0, 3, "page_3")
+
+        v_scales = []
+        for a in range(PASSES):
+            picked = held([P, S], U8, f"v_scales{a}")
+            nc.vector.tensor_copy(out=picked[:], in_=tab_planes[:, a, :].indirect(idx[:]))
+            v_scales.append(picked)
+        v_first = held([P, S], U32, "v_first")
+        nc.vector.tensor_copy(out=v_first[:], in_=table[0][:].indirect(idx[:]))
+        v_codes = {}
+        for h in range(HALVES):
+            v_codes[0, h] = v_first[:, h * BANK : (h + 1) * BANK]
+            picked = held([P, BANK], U32, f"v_second{h}")
+            nc.vector.tensor_copy(out=picked[:], in_=table[1][:].indirect(entries(idx, h * BANK, BANK)))
+            v_codes[1, h] = picked[:]
+
+        w1_op = {}
+
+        def quantise_w1(part, first_tile):
+            raw = w1_raw[part]
+            count = raw.shape[3]
+            grouped = held([P, PASSES, count, PACK], BF16, f"w1_grouped{part}")
+            for a in range(PASSES):
+                interleave(grouped[:, a], raw[:, a])
+            codes, scales = quantise(grouped[:].rearrange("p a c i -> p (a c i)"), PASSES * count, f"w1_{part}")
+            for s in range(count // P):
+                for a in range(PASSES):
+                    cols = slice(a * count + s * P, a * count + (s + 1) * P)
+                    w1_op[first_tile + s, a] = (codes[:, cols].bitcast(FP8X4), scales[:, cols])
+
+        def packed_op(first, rest, planes, per_col, dtype, t, a):
+            tile, s = (first, 0) if t == 0 else (rest, t - 1)
+            return (
+                tile[:, a, s * P * per_col : (s + 1) * P * per_col].bitcast(dtype),
+                planes[:, a, t * P : (t + 1) * P],
+            )
+
+        def reading(acc, ops, h):
+            for a in range(PASSES):
+                codes, scales = ops[a]
+                nc.tensor.matmul_mx(
+                    out=acc[:], lhsT=codes, lhsT_scale=scales,
+                    rhs=v_codes[a, h].bitcast(FP8X4), rhs_scale=v_scales[a][:, h * BANK : (h + 1) * BANK],
+                    start=(a == 0), stop=(a == PASSES - 1),
+                )
+
+        def largest_reading(best, t, halves):
+            partial, flood = {}, {}
+            for h in halves:
+                ebb = bank(h, "ebb")
+                reading(ebb, [packed_op(w2_first, w2_rest, w2_planes, 2, FP4X4, t, a) for a in range(PASSES)], h)
+                cross = bank(2 + h, "cross")
+                reading(cross, [packed_op(w3_first, w3_rest, w3_planes, 4, FP8X4, t, a) for a in range(PASSES)], h)
+                acc = bank(4 + h, "flood")
+                reading(acc, [w1_op[t, a] for a in range(PASSES)], h)
+                two = ring.tile([P, BANK], F32, name="two")
+                nc.scalar.copy(out=two[:], in_=ebb[:])
+                nc.vector.tensor_tensor(out=two[:], in0=cross[:], in1=two[:], op=ALU.max)
+                partial[h] = two
+                flood[h] = acc
+            for h in halves:
+                nc.vector.tensor_tensor(
+                    out=best[:, h * BANK : (h + 1) * BANK], in0=flood[h][:], in1=partial[h][:], op=ALU.max
+                )
+
+        def put(t, which, values, factors, first, count):
+            nc.vector.tensor_tensor(
+                out=page[t][:].indirect(entries(which, first, count)), in0=values, in1=factors, op=ALU.mult
+            )
+
+        def fetch(t, dst, first, count):
+            nc.vector.tensor_copy(out=dst, in_=page[t][:].indirect(entries(idx3, first, count)))
+
+        def subtract_turned(acc, t, fetched, first):
+            cols = slice(t * P, (t + 1) * P)
+            nc.tensor.matmul(
+                out=acc[:, cols], lhsT=neg_slack[t][:, first : first + P], rhs=ident[:],
+                is_transpose=True, start=True, stop=False,
+            )
+            nc.tensor.matmul(out=acc[:, cols], lhsT=fetched, rhs=ident[:], is_transpose=True, start=False, stop=True)
+
+        def turn_back(accs, word_bank, dst_words):
+            rounded = []
+            for acc in accs:
+                pairs = ring.tile([P, H], BF16, name="pairs", bufs=4)
+                nc.scalar.copy(
+                    out=pairs[:].rearrange("j (u p e) -> j u p e", u=2, e=2),
+                    in_=acc[:].rearrange("j (p u e) -> j u p e", u=2, e=2),
+                )
+                rounded.append(pairs)
+            words = bank(word_bank, "words")
+            for c, pairs in enumerate(rounded):
+                for u in range(2):
+                    nc.tensor.transpose(
+                        words[:, (2 * c + u) * P : (2 * c + u + 1) * P],
+                        pairs[:].bitcast(F32)[:, u * P : (u + 1) * P],
+                        ident[:],
+                    )
+            nc.scalar.copy(
+                out=dst_words.rearrange("p (c j u) -> p c j u", c=2, u=2),
+                in_=words[:].rearrange("p (c u j) -> p c j u", c=2, u=2),
+            )
+
+        quantise_w1(0, 0)
+        x_first = [bank(6 + c, "x_first") for c in range(FIRST // P)]
+        for t in range(TILES):
+            best = ring.tile([P, S], F32, name="best")
+            if t == 0:
+                largest_reading(best, t, [0])
+                put(t, idx2, best[:, :BANK], wgs_sb[:, :BANK], 0, BANK)
+                largest_reading(best, t, [1])
+                quantise_w1(1, 1)
+                put(t, idx2, best[:, BANK:], wgs_sb[:, BANK:], BANK, BANK)
+                quantise_w1(2, 2)
+            else:
+                largest_reading(best, t, range(HALVES))
+                put(t, idx2, best[:], wgs_sb[:], 0, S)
+            nc.scalar.activation(out=neg_slack[t][:], in_=neg_slack[t][:], func=ACT.Copy, scale=-1.0)
+            fetched = held([P, FIRST], F32, f"fetched_first{t}")
+            fetch(t, fetched[:], 0, FIRST)
+            for c in range(FIRST // P):
+                subtract_turned(x_first[c], t, fetched[:, c * P : (c + 1) * P], c * P)
+            if t == 1:
+                w4_grouped = held([P, H, PACK], BF16, "w4_grouped")
+                interleave(w4_grouped[:], w4_raw[:])
+                w4_codes, w4_scales = quantise(w4_grouped[:].rearrange("p n i -> p (n i)"), H, "w4")
+            if t == 2:
+                factor = held([P, TILES, J], F32, "factor")
+                for s in range(TILES):
+                    nc.scalar.activation(
+                        out=factor[:, s, :], in_=wgo_sb[:], func=ACT.Copy, scale=gain_sb[:, s : s + 1]
+                    )
+
+        def sizes(codes, scales, width, banks, name, tags):
+            per_bank = BANK // width
+            result = []
+            for g, b in enumerate(banks):
+                acc = bank(b, "score")
+                for s in range(per_bank):
+                    cols = slice((g * per_bank + s) * P, (g * per_bank + s + 1) * P)
+                    nc.tensor.matmul_mx(
+                        out=acc[:, s * width : (s + 1) * width],
+                        lhsT=w4_codes[:, cols].bitcast(FP8X4), lhsT_scale=w4_scales[:, cols],
+                        rhs=codes[:].bitcast(FP8X4), rhs_scale=scales[:], start=True, stop=True,
+                    )
+                size = held([P, BANK], F32, f"{name}{g}", tags[g])
+                nc.scalar.activation(out=size[:], in_=acc[:], func=ACT.Abs)
+                result.extend(size[:, s * width : (s + 1) * width] for s in range(per_bank))
+            return result
+
+        def rewrite(t, values, first, count):
+            put(t, idx4, values[t], factor[:, t, first : first + count], first, count)
+
+        x0 = held([P, FIRST * PACK], BF16, "x0", "after_first_quantise")
+        turn_back(x_first, 6, x0[:].bitcast(F32))
+
+        x_rest = [bank(c, "x_rest") for c in range(REST // P)]
+        fetched_rest = held([P, TILES - 1, REST], F32, "fetched_rest", "after_first_writing")
+        for t in range(TILES - 1):
+            fetch(t, fetched_rest[:, t, :], FIRST, REST)
+            for c in range(REST // P):
+                subtract_turned(x_rest[c], t, fetched_rest[:, t, c * P : (c + 1) * P], FIRST + c * P)
+        x0_codes, x0_scales = quantise(x0[:], FIRST, "x0")
+        size0 = sizes(x0_codes, x0_scales, FIRST, [7, 6], "size0_", ["before_x1", None])
+        fetched_last = held([P, REST], F32, "fetched_last", "after_first_quantise")
+        fetch(TILES - 1, fetched_last[:], FIRST, REST)
+        for c in range(REST // P):
+            subtract_turned(x_rest[c], TILES - 1, fetched_last[:, c * P : (c + 1) * P], FIRST + c * P)
+
+        x1 = held([P, FIRST * PACK], BF16, "x1")
+        turn_back(x_rest[0:2], 0, x1[:].bitcast(F32))
+        x2 = held([P, BANK * PACK], BF16, "x2")
+        turn_back(x_rest[2:4], 2, x2[:].bitcast(F32)[:, :BANK])
+        turn_back(x_rest[4:6], 4, x2[:].bitcast(F32)[:, BANK:])
+
+        for t in range(2):
+            rewrite(t, size0, 0, FIRST)
+        x1_codes, x1_scales = quantise(x1[:], FIRST, "x1", "before_x1")
+        size1 = sizes(x1_codes, x1_scales, FIRST, [1, 7], "size1_", ["before_x2", None])
+        for t in range(2, TILES):
+            rewrite(t, size0, 0, FIRST)
+        for t in range(2):
+            rewrite(t, size1, FIRST, FIRST)
+        x2_codes, x2_scales = quantise(x2[:], BANK, "x2", "before_x2")
+        size2 = sizes(x2_codes, x2_scales, BANK, [3, 5, 6, 0], "size2_", [None] * TILES)
+        for t in range(2, TILES):
+            rewrite(t, size1, FIRST, FIRST)
+        for t in range(TILES):
+            rewrite(t, size2, BANK, BANK)
+            nc.sync.dma_start(out=out[t * P : (t + 1) * P, :], in_=page[t][:])

@@ -107,9 +107,9 @@ def tile_list_wake_loading_page_kernel(
                 in_=dram.rearrange("a (q r) c -> r (a q) c", r=4).bitcast(I32),
             )
         idx2 = load_list(offs2, "idx2")
-        w1_raw = [load_w1(0, P)]
-        w3_first = load_words(w3_flat, 4, 0, P, "w3_first")
         w2_first = load_words(w2_words, 2, 0, P, "w2_first")
+        w3_first = load_words(w3_flat, 4, 0, P, "w3_first")
+        w1_raw = [load_w1(0, P)]
         tab_planes = load_planes(nc.sync, nc.vector, tab_scales, "tab_planes")
         w_planes = held([P, 2, PASSES, H], U8, "w_planes")
         nc.vector.memset(w_planes[:].rearrange("p w a c -> p (w a c)").bitcast(I32), 0)
@@ -141,18 +141,18 @@ def tile_list_wake_loading_page_kernel(
         nc.sync.dma_start(out=wgs_sb[:, BANK:], in_=wgs[:, BANK:])
         idx3 = load_list(offs3, "idx3")
         w1_raw.append(load_w1(2 * P, 2 * P))
-        page[1] = load_rows(page0, 1, "page_1")
         neg_slack[0] = load_rows(slack, 0, "slack_0")
+        page[1] = load_rows(page0, 1, "page_1")
         w4_raw = held([P, PACK, H], F32, "w4_raw")
         nc.sync.dma_start(out=w4_raw[:], in_=w4.rearrange("(p i) n -> p i n", i=PACK))
-        page[2] = load_rows(page0, 2, "page_2")
-        for t in range(1, TILES):
-            neg_slack[t] = load_rows(slack, t, f"slack_{t}")
         wgo_sb = load_rows(wgo, 0, "wgo_sb")
-        idx4 = load_list(offs4, "idx4")
         gain_sb = held([P, TILES], F32, "gain_sb")
         with nc.allow_non_contiguous_dma(reason="one gain a partition and row tile"):
             nc.sync.dma_start(out=gain_sb[:], in_=gain.rearrange("(t p) -> p t", p=P))
+        page[2] = load_rows(page0, 2, "page_2")
+        for t in range(1, TILES):
+            neg_slack[t] = load_rows(slack, t, f"slack_{t}")
+        idx4 = load_list(offs4, "idx4")
         page[3] = load_rows(page0, 3, "page_3")
 
         v_scales = []
@@ -200,7 +200,7 @@ def tile_list_wake_loading_page_kernel(
                 )
 
         def largest_reading(best, t, halves):
-            partial, flood = {}, {}
+            flood = {}
             for h in halves:
                 ebb = bank(h, "ebb")
                 reading(ebb, [packed_op(w2_first, w2_rest, w2_planes, 2, FP4X4, t, a) for a in range(PASSES)], h)
@@ -210,13 +210,13 @@ def tile_list_wake_loading_page_kernel(
                 reading(acc, [w1_op[t, a] for a in range(PASSES)], h)
                 two = ring.tile([P, BANK], F32, name="two")
                 nc.scalar.copy(out=two[:], in_=ebb[:])
-                nc.vector.tensor_tensor(out=two[:], in0=cross[:], in1=two[:], op=ALU.max)
-                partial[h] = two
+                nc.vector.tensor_tensor(
+                    out=best[:, h * BANK : (h + 1) * BANK], in0=cross[:], in1=two[:], op=ALU.max
+                )
                 flood[h] = acc
             for h in halves:
-                nc.vector.tensor_tensor(
-                    out=best[:, h * BANK : (h + 1) * BANK], in0=flood[h][:], in1=partial[h][:], op=ALU.max
-                )
+                cols = slice(h * BANK, (h + 1) * BANK)
+                nc.vector.tensor_tensor(out=best[:, cols], in0=flood[h][:], in1=best[:, cols], op=ALU.max)
 
         def put(t, which, values, factors, first, count):
             nc.vector.tensor_tensor(
@@ -258,6 +258,14 @@ def tile_list_wake_loading_page_kernel(
 
         quantise_w1(0, 0)
         x_first = [bank(6 + c, "x_first") for c in range(FIRST // P)]
+
+        def fetch_first(t):
+            nc.scalar.activation(out=neg_slack[t][:], in_=neg_slack[t][:], func=ACT.Copy, scale=-1.0)
+            fetched = held([P, FIRST], F32, f"fetched_first{t}")
+            fetch(t, fetched[:], 0, FIRST)
+            for c in range(FIRST // P):
+                subtract_turned(x_first[c], t, fetched[:, c * P : (c + 1) * P], c * P)
+
         for t in range(TILES):
             best = ring.tile([P, S], F32, name="best")
             if t == 0:
@@ -269,22 +277,18 @@ def tile_list_wake_loading_page_kernel(
                 quantise_w1(2, 2)
             else:
                 largest_reading(best, t, range(HALVES))
+                fetch_first(t - 1)
                 put(t, idx2, best[:], wgs_sb[:], 0, S)
-            nc.scalar.activation(out=neg_slack[t][:], in_=neg_slack[t][:], func=ACT.Copy, scale=-1.0)
-            fetched = held([P, FIRST], F32, f"fetched_first{t}")
-            fetch(t, fetched[:], 0, FIRST)
-            for c in range(FIRST // P):
-                subtract_turned(x_first[c], t, fetched[:, c * P : (c + 1) * P], c * P)
             if t == 1:
                 w4_grouped = held([P, H, PACK], BF16, "w4_grouped")
                 interleave(w4_grouped[:], w4_raw[:])
                 w4_codes, w4_scales = quantise(w4_grouped[:].rearrange("p n i -> p (n i)"), H, "w4")
-            if t == 2:
                 factor = held([P, TILES, J], F32, "factor")
                 for s in range(TILES):
                     nc.scalar.activation(
                         out=factor[:, s, :], in_=wgo_sb[:], func=ACT.Copy, scale=gain_sb[:, s : s + 1]
                     )
+        fetch_first(TILES - 1)
 
         def sizes(codes, scales, width, banks, name, tags):
             per_bank = BANK // width
@@ -310,20 +314,24 @@ def tile_list_wake_loading_page_kernel(
         turn_back(x_first, 6, x0[:].bitcast(F32))
 
         x_rest = [bank(c, "x_rest") for c in range(REST // P)]
-        fetched_rest = held([P, TILES - 1, REST], F32, "fetched_rest", "after_first_writing")
-        for t in range(TILES - 1):
-            fetch(t, fetched_rest[:, t, :], FIRST, REST)
-            for c in range(REST // P):
-                subtract_turned(x_rest[c], t, fetched_rest[:, t, c * P : (c + 1) * P], FIRST + c * P)
-        x0_codes, x0_scales = quantise(x0[:], FIRST, "x0")
-        size0 = sizes(x0_codes, x0_scales, FIRST, [7, 6], "size0_", ["before_x1", None])
-        fetched_last = held([P, REST], F32, "fetched_last", "after_first_quantise")
-        fetch(TILES - 1, fetched_last[:], FIRST, REST)
-        for c in range(REST // P):
-            subtract_turned(x_rest[c], TILES - 1, fetched_last[:, c * P : (c + 1) * P], FIRST + c * P)
 
+        def fetch_and_turn(t, dst, first, count):
+            fetch(t, dst, first, count)
+            for c in range(count // P):
+                subtract_turned(x_rest[(first - FIRST) // P + c], t, dst[:, c * P : (c + 1) * P], first + c * P)
+
+        fetched_mid = held([P, TILES * FIRST + 2 * BANK], F32, "fetched_mid", "after_first_writing")
+        for t in range(TILES):
+            fetch_and_turn(t, fetched_mid[:, t * FIRST : (t + 1) * FIRST], FIRST, FIRST)
         x1 = held([P, FIRST * PACK], BF16, "x1")
         turn_back(x_rest[0:2], 0, x1[:].bitcast(F32))
+        for t in range(2):
+            fetch_and_turn(t, fetched_mid[:, (2 + t) * BANK : (3 + t) * BANK], BANK, BANK)
+        x0_codes, x0_scales = quantise(x0[:], FIRST, "x0")
+        size0 = sizes(x0_codes, x0_scales, FIRST, [7, 6], "size0_", ["before_x1", None])
+        fetched_last = held([P, 2, BANK], F32, "fetched_last", "after_first_quantise")
+        for t in range(2, TILES):
+            fetch_and_turn(t, fetched_last[:, t - 2, :], BANK, BANK)
         x2 = held([P, BANK * PACK], BF16, "x2")
         turn_back(x_rest[2:4], 2, x2[:].bitcast(F32)[:, :BANK])
         turn_back(x_rest[4:6], 4, x2[:].bitcast(F32)[:, BANK:])

from contextlib import ExitStack

import concourse.mybir as mybir
from concourse.masks import make_identity

K, H, T, S, T2, J = 1024, 512, 4096, 1024, 2048, 1024
FLOPS = 2 * (3 * K * H * S + H * H * J)

F32 = mybir.dt.float32
BF16 = mybir.dt.bfloat16
I32 = mybir.dt.int32
U32 = mybir.dt.uint32
U16 = mybir.dt.uint16
U8 = mybir.dt.uint8
FP8X4 = mybir.dt.float8_e4m3fn_x4
FP4X4 = mybir.dt.float4_e2m1fn_x4
ALU = mybir.AluOpType
ACT = mybir.ActivationFunctionType

P = 128
PACK = 4
PASSES = K // (P * PACK)
TILES = H // P
BANK = 512
HALVES = S // BANK
PER_COL = 16
FIRST = 256
REST = J - FIRST


def tile_list_wake_loading_page_kernel(
    tc, tab_words, tab_scales, offs, offs2, offs3, offs4, w1, w2_words, w2_scales,
    w3_words, w3_scales, w4, page0, slack, gain, wgs, wgo, out,
):
    nc = tc.nc
    with ExitStack() as ctx:
        lists = ctx.enter_context(tc.tile_pool(name="lists", bufs=1))
        keep = ctx.enter_context(tc.tile_pool(name="keep", bufs=1))
        ring = ctx.enter_context(tc.tile_pool(name="ring", bufs=2))
        psum = ctx.enter_context(tc.psum_pool(name="psum", bufs=1))

        def held(shape, dtype, name, tag=None):
            return keep.tile(shape, dtype, name=name, tag=tag or name, align_bytes=64)

        def bank(b, name):
            return psum.tile([P, BANK], F32, name=name, tag=f"bank{b}")

        def load_list(dram, name):
            tile = lists.tile([P, dram.shape[1]], U16, name=name)
            nc.sync.dma_start(tile[:], dram)
            return tile

        def entries(tile, first, count):
            if count == tile.shape[1] * PER_COL:
                return tile[:]
            return tile[:, first // PER_COL : (first + count) // PER_COL]

        def load_planes(queue, zeroing, dram, name):
            width = dram.shape[2]
            tile = held([P, PASSES, width], U8, name)
            zeroing.memset(tile[:].bitcast(I32), 0)
            for q in range(4):
                queue.dma_start(
                    out=tile[32 * q : 32 * q + 4].bitcast(I32),
                    in_=dram[:, 4 * q : 4 * q + 4, :].rearrange("a r c -> r a c").bitcast(I32),
                )
            return tile

        def load_w1(first, count):
            raw = held([P, PASSES, PACK, count], F32, f"w1_raw{first}")
            for a in range(PASSES):
                rows = w1[a * P * PACK : (a + 1) * P * PACK, first : first + count]
                nc.sync.dma_start(out=raw[:, a], in_=rows.rearrange("(p i) c -> p i c", i=PACK))
            return raw

        def load_words(dram, per_col, first, count, name):
            tile = held([P, PASSES, count * per_col], U8, name)
            nc.sync.dma_start(
                out=tile[:].bitcast(I32),
                in_=dram[:, :, first * per_col : (first + count) * per_col].rearrange("a p c -> p a c").bitcast(I32),
            )
            return tile

        def load_rows(dram, t, name):
            tile = held([P, dram.shape[1]], F32, name)
            nc.sync.dma_start(out=tile[:], in_=dram[t * P : (t + 1) * P, :])
            return tile

        def interleave(dst, src):
            nc.scalar.copy(
                out=dst.rearrange("p (c n) i -> p c i n", n=4),
                in_=src.rearrange("p i (c n) -> p c i n", n=4),
            )

        def quantise(grouped, width, name, tag=None):
            codes = held([P, width], U32, name + "_codes", tag)
            scales = held([P, width], U8, name + "_scales")
            nc.vector.quantize_mx(out=codes[:].bitcast(FP8X4), scales=scales[:], in_=grouped)
            return codes, scales

        w3_flat = w3_words.rearrange("a p c i -> a p (c i)")
        idx = load_list(offs, "idx")
        w_rows = held([4, 2, PASSES, 4, H], U8, "w_rows")
        for w, dram in enumerate((w2_scales, w3_scales)):
            nc.sync.dma_start(
                out=w_rows[:, w].rearrange("r a q c -> r (a q) c").bitcast(I32),
                in_=dram.rearrange("a (q r) c -> r (a q) c", r=4).bitcast(I32),
            )
        idx2 = load_list(offs2, "idx2")
        w2_first = load_words(w2_words, 2, 0, P, "w2_first")
        w3_first = load_words(w3_flat, 4, 0, P, "w3_first")
        w1_raw = [load_w1(0, P)]
        tab_planes = load_planes(nc.sync, nc.vector, tab_scales, "tab_planes")
        w_planes = held([P, 2, PASSES, H], U8, "w_planes")
        nc.vector.memset(w_planes[:].rearrange("p w a c -> p (w a c)").bitcast(I32), 0)
        for q in range(4):
            nc.vector.tensor_copy(
                out=w_planes[32 * q : 32 * q + 4].rearrange("r w a c -> r (w a) c").bitcast(I32),
                in_=w_rows[:, :, :, q, :].rearrange("r w a c -> r (w a) c").bitcast(I32),
            )
        w2_planes, w3_planes = w_planes[:, 0], w_planes[:, 1]
        ident = held([P, P], F32, "ident")
        make_identity(nc, ident[:])

        table = []
        for a in range(PASSES):
            words = held([P, T], U32, f"table{a}")
            nc.sync.dma_start(
                out=words[:].bitcast(I32), in_=tab_words[a].rearrange("p t i -> p (t i)").bitcast(I32)
            )
            table.append(words)

        page = [None] * TILES
        neg_slack = [None] * TILES
        page[0] = load_rows(page0, 0, "page_0")
        wgs_sb = held([P, S], F32, "wgs_sb", "after_first_writing")
        nc.sync.dma_start(out=wgs_sb[:, :BANK], in_=wgs[:, :BANK])
        w1_raw.append(load_w1(P, P))
        w3_rest = load_words(w3_flat, 4, P, H - P, "w3_rest")
        w2_rest = load_words(w2_words, 2, P, H - P, "w2_rest")
        nc.sync.dma_start(out=wgs_sb[:, BANK:], in_=wgs[:, BANK:])
        idx3 = load_list(offs3, "idx3")
        w1_raw.append(load_w1(2 * P, 2 * P))
        neg_slack[0] = load_rows(slack, 0, "slack_0")
        page[1] = load_rows(page0, 1, "page_1")
        w4_raw = held([P, PACK, H], F32, "w4_raw")
        nc.sync.dma_start(out=w4_raw[:], in_=w4.rearrange("(p i) n -> p i n", i=PACK))
        wgo_sb = load_rows(wgo, 0, "wgo_sb")
        gain_sb = held([P, TILES], F32, "gain_sb")
        with nc.allow_non_contiguous_dma(reason="one gain a partition and row tile"):
            nc.sync.dma_start(out=gain_sb[:], in_=gain.rearrange("(t p) -> p t", p=P))
        page[2] = load_rows(page0, 2, "page_2")
        for t in range(1, TILES):
            neg_slack[t] = load_rows(slack, t, f"slack_{t}")
        idx4 = load_list(offs4, "idx4")
        page[3] = load_rows(page0, 3, "page_3")

        v_scales = []
        for a in range(PASSES):
            picked = held([P, S], U8, f"v_scales{a}")
            nc.vector.tensor_copy(out=picked[:], in_=tab_planes[:, a, :].indirect(idx[:]))
            v_scales.append(picked)
        v_first = held([P, S], U32, "v_first")
        nc.vector.tensor_copy(out=v_first[:], in_=table[0][:].indirect(idx[:]))
        v_codes = {}
        for h in range(HALVES):
            v_codes[0, h] = v_first[:, h * BANK : (h + 1) * BANK]
            picked = held([P, BANK], U32, f"v_second{h}")
            nc.vector.tensor_copy(out=picked[:], in_=table[1][:].indirect(entries(idx, h * BANK, BANK)))
            v_codes[1, h] = picked[:]

        w1_op = {}

        def quantise_w1(part, first_tile):
            raw = w1_raw[part]
            count = raw.shape[3]
            grouped = held([P, PASSES, count, PACK], BF16, f"w1_grouped{part}")
            for a in range(PASSES):
                interleave(grouped[:, a], raw[:, a])
            codes, scales = quantise(grouped[:].rearrange("p a c i -> p (a c i)"), PASSES * count, f"w1_{part}")
            for s in range(count // P):
                for a in range(PASSES):
                    cols = slice(a * count + s * P, a * count + (s + 1) * P)
                    w1_op[first_tile + s, a] = (codes[:, cols].bitcast(FP8X4), scales[:, cols])

        def packed_op(first, rest, planes, per_col, dtype, t, a):
            tile, s = (first, 0) if t == 0 else (rest, t - 1)
            return (
                tile[:, a, s * P * per_col : (s + 1) * P * per_col].bitcast(dtype),
                planes[:, a, t * P : (t + 1) * P],
            )

        def reading(acc, ops, h):
            for a in range(PASSES):
                codes, scales = ops[a]
                nc.tensor.matmul_mx(
                    out=acc[:], lhsT=codes, lhsT_scale=scales,
                    rhs=v_codes[a, h].bitcast(FP8X4), rhs_scale=v_scales[a][:, h * BANK : (h + 1) * BANK],
                    start=(a == 0), stop=(a == PASSES - 1),
                )

        def largest_reading(best, t, halves):
            flood = {}
            for h in halves:
                ebb = bank(h, "ebb")
                reading(ebb, [packed_op(w2_first, w2_rest, w2_planes, 2, FP4X4, t, a) for a in range(PASSES)], h)
                cross = bank(2 + h, "cross")
                reading(cross, [packed_op(w3_first, w3_rest, w3_planes, 4, FP8X4, t, a) for a in range(PASSES)], h)
                acc = bank(4 + h, "flood")
                reading(acc, [w1_op[t, a] for a in range(PASSES)], h)
                two = ring.tile([P, BANK], F32, name="two")
                nc.scalar.copy(out=two[:], in_=ebb[:])
                nc.vector.tensor_tensor(
                    out=best[:, h * BANK : (h + 1) * BANK], in0=cross[:], in1=two[:], op=ALU.max
                )
                flood[h] = acc
            for h in halves:
                cols = slice(h * BANK, (h + 1) * BANK)
                nc.vector.tensor_tensor(out=best[:, cols], in0=flood[h][:], in1=best[:, cols], op=ALU.max)

        def put(t, which, values, factors, first, count):
            nc.vector.tensor_tensor(
                out=page[t][:].indirect(entries(which, first, count)), in0=values, in1=factors, op=ALU.mult
            )

        def fetch(t, dst, first, count):
            nc.vector.tensor_copy(out=dst, in_=page[t][:].indirect(entries(idx3, first, count)))

        def subtract_turned(acc, t, fetched, first):
            cols = slice(t * P, (t + 1) * P)
            nc.tensor.matmul(
                out=acc[:, cols], lhsT=neg_slack[t][:, first : first + P], rhs=ident[:],
                is_transpose=True, start=True, stop=False,
            )
            nc.tensor.matmul(out=acc[:, cols], lhsT=fetched, rhs=ident[:], is_transpose=True, start=False, stop=True)

        def turn_back(accs, word_bank, dst_words):
            rounded = []
            for acc in accs:
                pairs = ring.tile([P, H], BF16, name="pairs", bufs=4)
                nc.scalar.copy(
                    out=pairs[:].rearrange("j (u p e) -> j u p e", u=2, e=2),
                    in_=acc[:].rearrange("j (p u e) -> j u p e", u=2, e=2),
                )
                rounded.append(pairs)
            words = bank(word_bank, "words")
            for c, pairs in enumerate(rounded):
                for u in range(2):
                    nc.tensor.transpose(
                        words[:, (2 * c + u) * P : (2 * c + u + 1) * P],
                        pairs[:].bitcast(F32)[:, u * P : (u + 1) * P],
                        ident[:],
                    )
            nc.scalar.copy(
                out=dst_words.rearrange("p (c j u) -> p c j u", c=2, u=2),
                in_=words[:].rearrange("p (c u j) -> p c j u", c=2, u=2),
            )

        quantise_w1(0, 0)
        x_first = [bank(6 + c, "x_first") for c in range(FIRST // P)]

        def fetch_first(t):
            nc.scalar.activation(out=neg_slack[t][:], in_=neg_slack[t][:], func=ACT.Copy, scale=-1.0)
            fetched = held([P, FIRST], F32, f"fetched_first{t}")
            fetch(t, fetched[:], 0, FIRST)
            for c in range(FIRST // P):
                subtract_turned(x_first[c], t, fetched[:, c * P : (c + 1) * P], c * P)

        for t in range(TILES):
            best = ring.tile([P, S], F32, name="best")
            if t == 0:
                largest_reading(best, t, [0])
                put(t, idx2, best[:, :BANK], wgs_sb[:, :BANK], 0, BANK)
                largest_reading(best, t, [1])
                quantise_w1(1, 1)
                put(t, idx2, best[:, BANK:], wgs_sb[:, BANK:], BANK, BANK)
                quantise_w1(2, 2)
            else:
                largest_reading(best, t, range(HALVES))
                fetch_first(t - 1)
                put(t, idx2, best[:], wgs_sb[:], 0, S)
            if t == 1:
                w4_grouped = held([P, H, PACK], BF16, "w4_grouped")
                interleave(w4_grouped[:], w4_raw[:])
                w4_codes, w4_scales = quantise(w4_grouped[:].rearrange("p n i -> p (n i)"), H, "w4")
                factor = held([P, TILES, J], F32, "factor")
                for s in range(TILES):
                    nc.scalar.activation(
                        out=factor[:, s, :], in_=wgo_sb[:], func=ACT.Copy, scale=gain_sb[:, s : s + 1]
                    )
        fetch_first(TILES - 1)

        def sizes(codes, scales, width, banks, name, tags):
            per_bank = BANK // width
            result = []
            for g, b in enumerate(banks):
                acc = bank(b, "score")
                for s in range(per_bank):
                    cols = slice((g * per_bank + s) * P, (g * per_bank + s + 1) * P)
                    nc.tensor.matmul_mx(
                        out=acc[:, s * width : (s + 1) * width],
                        lhsT=w4_codes[:, cols].bitcast(FP8X4), lhsT_scale=w4_scales[:, cols],
                        rhs=codes[:].bitcast(FP8X4), rhs_scale=scales[:], start=True, stop=True,
                    )
                size = held([P, BANK], F32, f"{name}{g}", tags[g])
                nc.scalar.activation(out=size[:], in_=acc[:], func=ACT.Abs)
                result.extend(size[:, s * width : (s + 1) * width] for s in range(per_bank))
            return result

        def rewrite(t, values, first, count):
            put(t, idx4, values[t], factor[:, t, first : first + count], first, count)

        x0 = held([P, FIRST * PACK], BF16, "x0", "after_first_quantise")
        turn_back(x_first, 6, x0[:].bitcast(F32))

        x_rest = [bank(c, "x_rest") for c in range(REST // P)]

        def fetch_and_turn(t, dst, first, count):
            fetch(t, dst, first, count)
            for c in range(count // P):
                subtract_turned(x_rest[(first - FIRST) // P + c], t, dst[:, c * P : (c + 1) * P], first + c * P)

        fetched_mid = held([P, TILES * FIRST + 2 * BANK], F32, "fetched_mid", "after_first_writing")
        for t in range(TILES):
            fetch_and_turn(t, fetched_mid[:, t * FIRST : (t + 1) * FIRST], FIRST, FIRST)
        x1 = held([P, FIRST * PACK], BF16, "x1")
        turn_back(x_rest[0:2], 0, x1[:].bitcast(F32))
        for t in range(2):
            fetch_and_turn(t, fetched_mid[:, (2 + t) * BANK : (3 + t) * BANK], BANK, BANK)
        x0_codes, x0_scales = quantise(x0[:], FIRST, "x0")
        size0 = sizes(x0_codes, x0_scales, FIRST, [7, 6], "size0_", ["before_x1", None])
        fetched_last = held([P, 2, BANK], F32, "fetched_last", "after_first_quantise")
        for t in range(2, TILES):
            fetch_and_turn(t, fetched_last[:, t - 2, :], BANK, BANK)
        x2 = held([P, BANK * PACK], BF16, "x2")
        turn_back(x_rest[2:4], 2, x2[:].bitcast(F32)[:, :BANK])
        turn_back(x_rest[4:6], 4, x2[:].bitcast(F32)[:, BANK:])

        for t in range(2):
            rewrite(t, size0, 0, FIRST)
        x1_codes, x1_scales = quantise(x1[:], FIRST, "x1", "before_x1")
        size1 = sizes(x1_codes, x1_scales, FIRST, [1, 7], "size1_", ["before_x2", None])
        for t in range(2, TILES):
            rewrite(t, size0, 0, FIRST)
        for t in range(2):
            rewrite(t, size1, FIRST, FIRST)
        x2_codes, x2_scales = quantise(x2[:], BANK, "x2", "before_x2")
        size2 = sizes(x2_codes, x2_scales, BANK, [3, 5, 6, 0], "size2_", [None] * TILES)
        for t in range(2, TILES):
            rewrite(t, size1, FIRST, FIRST)
        for t in range(TILES):
            rewrite(t, size2, BANK, BANK)
            nc.sync.dma_start(out=out[t * P : (t + 1) * P, :], in_=page[t][:])
